import numpy as np
import ml_dtypes


def mxq(x, axis, fmt="e4m3"):
    dtype, down = {"e4m3": (ml_dtypes.float8_e4m3fn, 7), "e5m2": (ml_dtypes.float8_e5m2, 14)}[fmt]
    v = np.moveaxis(np.asarray(x, np.float32).astype(ml_dtypes.bfloat16).astype(np.float64), axis, -1)
    blocks = v.reshape(v.shape[:-1] + (-1, 32))
    amax = np.abs(blocks).max(-1, keepdims=True)
    byte = np.maximum(np.where(amax > 0, np.frexp(amax)[1] - 1 + 127, 0) - down, 1)
    scale = np.exp2(byte - 127.0)
    codes = (blocks / scale).astype(np.float32).astype(dtype).astype(np.float64)
    return np.moveaxis((codes * scale).reshape(v.shape), -1, axis)


WIDE = False


def mx_kscale(k):
    if not WIDE:
        return np.ones(k)
    levels = np.array([10, -10, 5, -5, 0])
    if k % 512:
        return np.exp2(np.random.permutation(np.resize(levels, k // 32))).repeat(32)
    a = np.empty((k // 512, 16))
    for p in range(k // 512):
        a[p, :8] = np.random.permutation(np.resize(levels, 8))
        for g in range(8):
            far = levels[np.abs(levels - a[p, g]) >= 10]
            a[p, g + 8] = far[np.random.randint(len(far))]
    return np.exp2(a.ravel()).repeat(32)


def f64(x):
    return np.asarray(x).astype(np.float64)


def striped(idx):
    return np.tile(np.asarray(idx).reshape(-1, 16).T, (8, 1)).astype(np.uint16)


def unstriped(offs):
    return offs[:16].T.reshape(-1).astype(np.int64)


E2M1 = np.array([0.0, 0.5, 1.0, 1.5, 2.0, 3.0, 4.0, 6.0, -0.0, -0.5, -1.0, -1.5, -2.0, -3.0, -4.0, -6.0])


def pack_weight(w, fmt):
    k, n = w.shape
    w = f64(np.asarray(w, np.float32).astype(ml_dtypes.bfloat16)).reshape(k // 32, 32, n)
    amax = np.abs(w).max(1)
    if fmt == "e4m3":
        byte = np.frexp(amax)[1] - 1 + 127 - 7
    else:
        mant, ex = np.frexp(amax / 6.0)
        byte = np.where(mant > 0.5, ex, ex - 1) + 127
    byte = np.clip(np.where(amax > 0, byte, 1), 1, 254)
    scaled = (w * np.exp2(127.0 - byte)[:, None, :]).reshape(k, n).astype(np.float32)
    by_word = np.ascontiguousarray(scaled.reshape(k // 512, 128, 4, n).transpose(0, 1, 3, 2))
    if fmt == "e4m3":
        words = by_word.astype(ml_dtypes.float8_e4m3fn).view(np.uint8)
    else:
        c = by_word.astype(ml_dtypes.float4_e2m1fn).view(np.uint8) & 0xF
        words = (c[..., 0::2] | (c[..., 1::2] << 4)).reshape(k // 512, 128, 2 * n)
    return np.ascontiguousarray(words), np.ascontiguousarray(byte.astype(np.uint8).reshape(k // 512, 16, n))


def unpack_weight(words, scales, fmt):
    g, _, n = scales.shape
    words = np.ascontiguousarray(words).reshape(g, 128, n, -1)
    if fmt == "e4m3":
        vals = words.view(ml_dtypes.float8_e4m3fn).astype(np.float64)
    else:
        nib = np.empty((g, 128, n, 4), np.uint8)
        nib[..., 0::2] = words & 0xF
        nib[..., 1::2] = words >> 4
        vals = E2M1[nib]
    vals = vals * np.repeat(np.exp2(scales.astype(np.float64) - 127.0), 8, axis=1)[..., None]
    return vals.transpose(0, 1, 3, 2).reshape(g * 512, n)


def bf(x):
    return np.asarray(x, np.float32).astype(ml_dtypes.bfloat16)


def planes(Y):
    r, m = Y.shape
    b = f64(bf(Y)).reshape(r // 32, 32, m)
    amax = np.abs(b).max(1)
    byte = np.clip(np.where(amax > 0, np.frexp(amax)[1] - 1 + 127 - 7, 1), 1, 254)
    codes = (b * np.exp2(127.0 - byte)[:, None, :]).reshape(r, m).astype(np.float32).astype(ml_dtypes.float8_e4m3fn).view(np.uint8)
    words = codes.reshape(r // 512, 128, 4, m).transpose(0, 1, 3, 2)
    return np.ascontiguousarray(words), np.ascontiguousarray(byte.astype(np.uint8).reshape(r // 512, 16, m))


D, T, I, Q, E, V, G = 512, 2048, 512, 256, 512, 32, 64


def setup_inputs():
    n = np.random.standard_normal
    idx = np.random.permutation(T)[:I]
    fd = mx_kscale(D)
    fi = mx_kscale(I)
    ti = np.ones(T)
    ti[idx] = fi
    keysp = pack_weight(n((D, T)) / fd[:, None], "e2m1")
    return {
        "query": (n((D, Q)) * 0.52 / np.sqrt(D) * fd[:, None]).astype(np.float32),
        "keys_words": keysp[0],
        "keys_scales": keysp[1],
        "lam": (np.random.uniform(0.05, 0.12, (1, Q))).astype(np.float32),
        "bar": (np.random.uniform(0.6, 1.0, (Q, 1))).astype(np.float32),
        "reserve": (np.random.uniform(20.0, 80.0, (Q, 1))).astype(np.float32),
        "os": (np.random.uniform(4.0, 16.0, (1, I)) * fi).astype(np.float32),
        "vals": (n((E, T)) / ti).astype(np.float32),
        "before": (n((E, Q))).astype(np.float32),
        "hold": (np.random.uniform(0.1, 0.6, (1, Q))).astype(np.float32),
        "offs": striped(idx),
    }


def reference(query, keys_words, keys_scales, lam, bar, reserve, os, vals, before, hold, offs):
    idx = unstriped(offs)
    keysu = unpack_weight(keys_words, keys_scales, "e2m1")
    keysidxg = keysu[:, idx]
    queryq = mxq(f64(query), 0, "e4m3")
    a0 = keysidxg.T @ queryq
    ag = a0.reshape(I, V, Q // V).sum(axis=2)
    ar = np.repeat(ag, Q // V, axis=1)
    s0 = a0 - ar * f64(lam)
    s = s0.T
    p = np.exp(s)
    pm = p.reshape(Q, G, I // G).mean(axis=2)
    pr = np.repeat(pm, I // G, axis=1)
    r = np.maximum(p - pr * f64(bar), 0.0)
    w = r / (np.sum(r, axis=1, keepdims=True) + f64(reserve))
    wo1 = w * f64(os)
    wt1 = wo1.T
    vt1 = f64(vals)[:, idx].T
    vt1q = mxq(vt1, 0, "e4m3")
    wt1q = mxq(wt1, 0, "e4m3")
    o = vt1q.T @ wt1q
    y = f64(before) * f64(hold) + o * (1.0 - f64(hold))
    words, scales = planes(y)
    return y, words, scales

@@ -1,0 +1,299 @@
+from contextlib import ExitStack
+
+import concourse.mybir as mybir
+from concourse.masks import make_identity
+
+D, T, I, Q, E = 512, 2048, 512, 256, 512
+FLOPS = 2 * D * I * Q + 2 * I * E * Q
+
+F32 = mybir.dt.float32
+BF16 = mybir.dt.bfloat16
+I32 = mybir.dt.int32
+U32 = mybir.dt.uint32
+U16 = mybir.dt.uint16
+U8 = mybir.dt.uint8
+FP8X4 = mybir.dt.float8_e4m3fn_x4
+FP4X4 = mybir.dt.float4_e2m1fn_x4
+ALU = mybir.AluOpType
+ACT = mybir.ActivationFunctionType
+AX = mybir.AxisListType
+
+P = 128
+PACK = 4
+GROUP = 8
+HALVES = Q // P
+
+
+def tile_attend_beyondgroup_abovepage_blend_pl_kernel(
+    tc, query, keys_words, keys_scales, lam, bar, reserve, slot_factor, vals, before, hold, offs, out_0, out_1, out_2
+):
+    nc = tc.nc
+    with ExitStack() as ctx:
+        sb = ctx.enter_context(tc.tile_pool(name="sb", bufs=1))
+        ps = ctx.enter_context(tc.psum_pool(name="ps", bufs=1))
+
+        def sbt(name, shape, dtype):
+            return sb.tile(shape, dtype, name=name, align_bytes=64)
+
+        def bank(name, tag, shape):
+            return ps.tile(shape, F32, name=name, tag=tag)
+
+        offsets = sb.tile([P, I // 16], U16, name="offsets")
+        key_words = sbt("key_words", [P, T], U16)
+        key_bytes = sbt("key_bytes", [P, T], U8)
+        rows = sbt("rows", [P, 2, P], F32)
+        q_raw = sbt("q_raw", [P, PACK, Q], F32)
+        before_sb = sbt("before_sb", [P, PACK, Q], F32)
+        val_pool = [sbt("val_pool%d" % j, [P, T], F32) for j in range(PACK)]
+        ident = sbt("ident", [P, P], F32)
+
+        nc.gpsimd.memset(key_bytes[:].bitcast(I32), 0)
+        nc.gpsimd.memset(rows[:], 0.0)
+        make_identity(nc, ident[:])
+
+        nc.sync.dma_start(offsets[:], offs)
+        nc.sync.dma_start(key_words[:].bitcast(I32), keys_words[0].bitcast(I32))
+        for quad in range(4):
+            nc.sync.dma_start(
+                key_bytes[32 * quad : 32 * quad + 4, :].bitcast(I32),
+                keys_scales[0, 4 * quad : 4 * quad + 4, :].bitcast(I32),
+            )
+        nc.sync.dma_start(q_raw[:], query.rearrange("(p j) q -> p j q", j=PACK))
+        vals_dealt = vals.rearrange("(p j) t -> p j t", j=PACK)
+        nc.sync.dma_start(rows[0:2, 0, :], lam.rearrange("o (u q) -> (o u) q", u=2))
+        nc.sync.dma_start(val_pool[0][:], vals_dealt[:, 0, :])
+        nc.sync.dma_start(rows[0:2, 1, :], bar.rearrange("(u q) o -> u (q o)", u=2))
+        nc.sync.dma_start(rows[2:4, 1, :], reserve.rearrange("(u q) o -> u (q o)", u=2))
+        nc.sync.dma_start(rows[4:8, 1, :], slot_factor.rearrange("o (u q) -> (o u) q", u=4))
+        nc.sync.dma_start(rows[8:10, 1, :], hold.rearrange("o (u q) -> (o u) q", u=2))
+        for j in range(1, PACK):
+            nc.sync.dma_start(val_pool[j][:], vals_dealt[:, j, :])
+        nc.sync.dma_start(before_sb[:], before.rearrange("(p j) q -> p j q", j=PACK))
+
+        keys_g = sbt("keys_g", [P, I], U16)
+        key_scale_g = sbt("key_scale_g", [P, I], U8)
+        nc.vector.tensor_copy(keys_g[:], key_words[:].indirect(offsets[:]))
+        nc.vector.tensor_copy(key_scale_g[:], key_bytes[:].indirect(offsets[:]))
+
+        lam_ps = bank("lam_ps", "vt0", [P, P])
+        nc.tensor.transpose(lam_ps[:], rows[:, 0, :], ident[:])
+        lam_cols = sbt("lam_cols", [P, HALVES], F32)
+        nc.scalar.copy(lam_cols[:], lam_ps[:, 0:HALVES])
+        lam_row = bank("lam_row", "lh", [P, Q])
+        for c in range(HALVES):
+            nc.tensor.transpose(lam_row[:, c * P : (c + 1) * P], lam_cols[:, c : c + 1].to_broadcast([P, P]), ident[:])
+
+        q_codes, q_scales = [], []
+        for u in range(HALVES):
+            q_bf = sbt("q_bf%d" % u, [P, P, PACK], BF16)
+            nc.scalar.copy(
+                q_bf[:].rearrange("p (c i) j -> p c j i", i=4),
+                q_raw[:, :, u * P : (u + 1) * P].rearrange("p j (c i) -> p c j i", i=4),
+            )
+            codes = sbt("q_codes%d" % u, [P, P], U32)
+            scales = sbt("q_scales%d" % u, [P, P], U8)
+            nc.vector.quantize_mx(codes[:].bitcast(FP8X4), scales[:], q_bf[:].rearrange("p q j -> p (q j)"))
+            q_codes.append(codes)
+            q_scales.append(scales)
+
+        raw_ps = []
+        for u in range(HALVES):
+            raw = bank("raw%d" % u, "a%d" % u, [P, PACK, P])
+            for t in range(PACK):
+                nc.tensor.matmul_mx(
+                    out=raw[:, t, :],
+                    lhsT=keys_g[:, t * P : (t + 1) * P].bitcast(FP4X4),
+                    lhsT_scale=key_scale_g[:, t * P : (t + 1) * P],
+                    rhs=q_codes[u][:].bitcast(FP8X4),
+                    rhs_scale=q_scales[u][:],
+                    start=True,
+                    stop=True,
+                )
+            raw_ps.append(raw)
+
+        val_codes, val_scales = {}, {}
+        runs = I // GROUP
+        share0 = sbt("share0", [P, I // 2], F32)
+        share2 = sbt("share2", [P, P + I], F32)
+        val_bf = [share0[:].bitcast(BF16), sbt("val_bf1", [P, I], BF16)[:], share2[:, 0 : I // 2].bitcast(BF16)]
+        val_bf.append(sbt("val_bf3", [P, I], BF16)[:])
+        neg_sums = [share0[:, P : P + runs], sbt("neg_sum1", [P, runs], F32)[:]]
+        shifts = [sbt("shift%d" % u, [P, I], F32)[:] for u in range(HALVES)]
+        aboves = [share2[:, P : P + I], sbt("above1", [P, I], F32)[:]]
+
+        def gather_values(j, part, engine):
+            n = I // 2
+            window = val_pool[j][:].indirect(offsets[:, part * n // 16 : (part + 1) * n // 16])
+            if engine == "scalar":
+                nc.scalar.activation(val_bf[j][:, part * n : (part + 1) * n], window, ACT.Copy)
+            else:
+                nc.vector.tensor_copy(val_bf[j][:, part * n : (part + 1) * n], window)
+
+        def turn_pairs(src, turned, grouped):
+            words = src.bitcast(F32)
+            for h in range(2):
+                nc.tensor.transpose(turned[:, h, :], words[:, h : I // 2 : 2], ident[:])
+            nc.scalar.copy(grouped[:].bitcast(F32), turned[:].rearrange("p h c -> p c h"))
+
+        def quantise_values(j):
+            turned = bank("val_turned%d" % j, "vt%d" % (j % 2), [P, 2, P])
+            grouped = sbt("val_grouped%d" % j, [P, P, PACK], BF16)
+            turn_pairs(val_bf[j], turned, grouped)
+            val_codes[j] = sbt("val_codes%d" % j, [P, P], U32)
+            val_scales[j] = sbt("val_scales%d" % j, [P, P], U8)
+            nc.vector.quantize_mx(
+                val_codes[j][:].bitcast(FP8X4), val_scales[j][:], grouped[:].rearrange("p c t -> p (c t)")
+            )
+
+        probs = []
+        for u in range(HALVES):
+            neg_sum = neg_sums[u]
+            nc.vector.tensor_reduce(
+                neg_sum, raw_ps[u][:].rearrange("p t (v c) -> p (t v) c", c=GROUP), AX.X, ALU.add, negate=True
+            )
+            raw_sb = sbt("raw_sb%d" % u, [P, PACK, P], F32)
+            nc.scalar.copy(raw_sb[:], raw_ps[u][:])
+            shift = shifts[u].rearrange("p (t q) -> p t q", t=PACK)
+            four_d = [P, PACK, P // GROUP, GROUP]
+            nc.vector.tensor_tensor(
+                shift.rearrange("p t (v c) -> p t v c", c=GROUP),
+                neg_sum.rearrange("p (t v) -> p t v", t=PACK).unsqueeze(3).to_broadcast(four_d),
+                lam_row[:, u * P : (u + 1) * P].rearrange("p (v c) -> p v c", c=GROUP).unsqueeze(1).to_broadcast(four_d),
+                ALU.mult,
+            )
+            score = bank("score%d" % u, "s%d" % u, [P, PACK, P])
+            for t in range(PACK):
+                nc.tensor.matmul(score[:, t, :], raw_sb[:, t, :], ident[:], start=(t == 0), stop=False, is_transpose=True)
+            order = list(range(PACK))
+            for t in order:
+                nc.tensor.matmul(
+                    score[:, t, :], shift[:, t, :], ident[:], start=False, stop=(t == order[-1]), is_transpose=True
+                )
+            prob = sbt("prob%d" % u, [P, I], F32)
+            nc.scalar.activation(prob[:], score[:].rearrange("p t s -> p (t s)"), ACT.Exp)
+            probs.append(prob)
+
+        for part in range(2):
+            gather_values(0, part, "scalar")
+        for part in range(2):
+            gather_values(1, part, "vector")
+
+        cols_ps = bank("cols_ps", "vt1", [P, P])
+        nc.tensor.transpose(cols_ps[:], rows[:, 1, :], ident[:])
+        cols = sbt("cols", [P, 10], F32)
+        nc.scalar.copy(cols[:], cols_ps[:, 0:10])
+        neg_bar = sbt("neg_bar", [P, HALVES], F32)
+        nc.scalar.activation(neg_bar[:], cols_ps[:, 0:2], ACT.Copy, scale=-1.0 / GROUP)
+        os_row = bank("os_row", "os", [P, I])
+        for c in range(4):
+            nc.tensor.transpose(os_row[:, c * P : (c + 1) * P], cols[:, 4 + c : 5 + c].to_broadcast([P, P]), ident[:])
+
+        w_codes = sbt("w_codes", [P, Q], U32)
+        w_scales = sbt("w_scales", [P, Q], U8)
+        for u in range(HALVES):
+            run_sum = sbt("run_sum%d" % u, [P, I // GROUP], F32)
+            prob_runs = probs[u][:].rearrange("p (g c) -> p g c", c=GROUP)
+            nc.vector.tensor_reduce(run_sum[:], prob_runs, AX.X, ALU.add)
+            above = aboves[u]
+            nc.vector.scalar_tensor_tensor(
+                above.rearrange("p (g c) -> p g c", c=GROUP),
+                run_sum[:].unsqueeze(2).to_broadcast([P, I // GROUP, GROUP]),
+                neg_bar[:, u : u + 1],
+                prob_runs,
+                ALU.mult,
+                ALU.add,
+            )
+            part_of = sbt("part_of%d" % u, [P, I], F32)
+            row_sum = sbt("row_sum%d" % u, [P, 1], F32)
+            nc.scalar.activation(part_of[:], above, ACT.Relu, accum_out=row_sum[:])
+            denom = sbt("denom%d" % u, [P, 1], F32)
+            nc.vector.tensor_tensor(denom[:], row_sum[:], cols[:, 2 + u : 3 + u], ALU.add)
+            inverse = sbt("inverse%d" % u, [P, 1], F32)
+            nc.vector.reciprocal(inverse[:], denom[:])
+            w_bf = sbt("w_bf%d" % u, [P, I], BF16)[:]
+            nc.vector.scalar_tensor_tensor(w_bf, part_of[:], inverse[:], os_row[:], ALU.mult, ALU.mult)
+            turned = bank("w_turned%d" % u, "s%d" % u, [P, 2, P])
+            grouped = sbt("w_grouped%d" % u, [P, P, PACK], BF16)
+            turn_pairs(w_bf, turned, grouped)
+            nc.vector.quantize_mx(
+                w_codes[:, u * P : (u + 1) * P].bitcast(FP8X4),
+                w_scales[:, u * P : (u + 1) * P],
+                grouped[:].rearrange("p c t -> p (c t)"),
+            )
+
+        for part in range(2):
+            gather_values(2, part, "scalar")
+        hold_ps = bank("hold_ps", "vt1", [P, Q])
+        for c in range(HALVES):
+            nc.tensor.transpose(hold_ps[:, c * P : (c + 1) * P], cols[:, 8 + c : 9 + c].to_broadcast([P, P]), ident[:])
+        hold_row = sbt("hold_row", [P, Q], F32)
+        nc.vector.tensor_copy(hold_row[:], hold_ps[:])
+        fresh_row = sbt("fresh_row", [P, Q], F32)
+        nc.gpsimd.tensor_scalar(fresh_row[:], hold_row[:], -1.0, 1.0, ALU.mult, ALU.add)
+        kept = sbt("kept", [P, PACK, Q], F32)
+        for u in range(HALVES):
+            qs = slice(u * P, (u + 1) * P)
+            nc.gpsimd.tensor_tensor(
+                kept[:, :, qs], before_sb[:, :, qs], hold_row[:, qs].unsqueeze(1).to_broadcast([P, PACK, P]), ALU.mult
+            )
+
+        quantise_values(0)
+        quantise_values(1)
+        quantise_values(2)
+        gather_values(3, 0, "vector")
+        gather_values(3, 1, "scalar")
+        quantise_values(3)
+
+        result = sbt("result", [P, PACK, Q], F32)
+        out_dealt = out_0.rearrange("(p j) q -> p j q", j=PACK)
+        last = PACK - 1
+        for u in range(HALVES):
+            qs = slice(u * P, (u + 1) * P)
+            read = bank("read%d" % u, "a%d" % u, [P, last, P])
+            for j in range(last):
+                nc.tensor.matmul_mx(
+                    out=read[:, j, :],
+                    lhsT=val_codes[j][:].bitcast(FP8X4),
+                    lhsT_scale=val_scales[j][:],
+                    rhs=w_codes[:, qs].bitcast(FP8X4),
+                    rhs_scale=w_scales[:, qs],
+                    start=True,
+                    stop=True,
+                )
+            fresh = sbt("fresh%d" % u, [P, last, P], F32)
+            nc.vector.tensor_tensor(fresh[:], read[:], fresh_row[:, qs].unsqueeze(1).to_broadcast([P, last, P]), ALU.mult)
+            nc.vector.tensor_tensor(result[:, 0:last, qs], fresh[:], kept[:, 0:last, qs], ALU.add)
+            nc.sync.dma_start(out_dealt[:, 0:last, qs], result[:, 0:last, qs])
+        read = bank("read_last", "lh", [P, Q])
+        nc.tensor.matmul_mx(
+            out=read[:],
+            lhsT=val_codes[last][:].bitcast(FP8X4),
+            lhsT_scale=val_scales[last][:],
+            rhs=w_codes[:].bitcast(FP8X4),
+            rhs_scale=w_scales[:],
+            start=True,
+            stop=True,
+        )
+        fresh = sbt("fresh_last", [P, Q], F32)
+        nc.vector.tensor_tensor(fresh[:], read[:], fresh_row[:], ALU.mult)
+        nc.vector.tensor_tensor(result[:, last, :], fresh[:], kept[:, last, :], ALU.add)
+        nc.sync.dma_start(out_dealt[:, last, :], result[:, last, :])
+
+        y_codes = sbt("y_codes", [P, Q], U32)
+        y_scales = sbt("y_scales", [P, Q], U8)
+        for u in range(HALVES):
+            qs = slice(u * P, (u + 1) * P)
+            y_bf = sbt("y_bf%d" % u, [P, P, PACK], BF16)
+            dst = y_bf[:].rearrange("p (c i) j -> p c j i", i=4)
+            src = result[:, :, qs].rearrange("p j (c i) -> p c j i", i=4)
+            if u == 0:
+                nc.vector.tensor_copy(dst, src)
+            else:
+                nc.scalar.copy(dst, src)
+            nc.vector.quantize_mx(y_codes[:, qs].bitcast(FP8X4), y_scales[:, qs], y_bf[:].rearrange("p q j -> p (q j)"))
+        nc.sync.dma_start(out_1[0].rearrange("p c r -> p (c r)").bitcast(I32), y_codes[:].bitcast(I32))
+        for quad in range(4):
+            engine = nc.sync if quad % 2 == 0 else nc.scalar
+            engine.dma_start(
+                out_2[0, 4 * quad : 4 * quad + 4, :].bitcast(I32), y_scales[32 * quad : 32 * quad + 4, :].bitcast(I32)
+            )

@@ -32,8 +32,8 @@ def tile_attend_beyondgroup_abovepage_blend_pl_kernel(
         sb = ctx.enter_context(tc.tile_pool(name="sb", bufs=1))
         ps = ctx.enter_context(tc.psum_pool(name="ps", bufs=1))
 
-        def sbt(name, shape, dtype):
-            return sb.tile(shape, dtype, name=name, align_bytes=64)
+        def sbt(name, shape, dtype, tag=None):
+            return sb.tile(shape, dtype, name=name, tag=tag or name, align_bytes=64)
 
         def bank(name, tag, shape):
             return ps.tile(shape, F32, name=name, tag=tag)
@@ -53,11 +53,8 @@ def tile_attend_beyondgroup_abovepage_blend_pl_kernel(
 
         nc.sync.dma_start(offsets[:], offs)
         nc.sync.dma_start(key_words[:].bitcast(I32), keys_words[0].bitcast(I32))
-        for quad in range(4):
-            nc.sync.dma_start(
-                key_bytes[32 * quad : 32 * quad + 4, :].bitcast(I32),
-                keys_scales[0, 4 * quad : 4 * quad + 4, :].bitcast(I32),
-            )
+        for r in range(4):
+            nc.sync.dma_start(key_bytes[r:P:32, :].bitcast(I32), keys_scales[0, r:16:4, :].bitcast(I32))
         nc.sync.dma_start(q_raw[:], query.rearrange("(p j) q -> p j q", j=PACK))
         vals_dealt = vals.rearrange("(p j) t -> p j t", j=PACK)
         nc.sync.dma_start(rows[0:2, 0, :], lam.rearrange("o (u q) -> (o u) q", u=2))
@@ -111,15 +108,18 @@ def tile_attend_beyondgroup_abovepage_blend_pl_kernel(
                 )
             raw_ps.append(raw)
 
-        val_codes, val_scales = {}, {}
         runs = I // GROUP
         share0 = sbt("share0", [P, I // 2], F32)
-        share2 = sbt("share2", [P, P + I], F32)
-        val_bf = [share0[:].bitcast(BF16), sbt("val_bf1", [P, I], BF16)[:], share2[:, 0 : I // 2].bitcast(BF16)]
-        val_bf.append(sbt("val_bf3", [P, I], BF16)[:])
+        share2 = sbt("share2", [P, I + P // 2], F32)
+        share3 = sbt("share3", [P, I], F32)
+        val_bf = [share0[:].bitcast(BF16), sbt("val_bf1", [P, I], BF16)[:]]
+        val_bf += [share2[:, I + P // 2 - I // 2 : I + P // 2].bitcast(BF16), share3[:, 0 : I // 2].bitcast(BF16)]
         neg_sums = [share0[:, P : P + runs], sbt("neg_sum1", [P, runs], F32)[:]]
-        shifts = [sbt("shift%d" % u, [P, I], F32)[:] for u in range(HALVES)]
-        aboves = [share2[:, P : P + I], sbt("above1", [P, I], F32)[:]]
+        shifts = [sbt("shift0", [P, I], F32)[:], share2[:, 0:I]]
+        aboves = [sbt("above0", [P, I], F32)[:], share3[:]]
+        w_bfs = [sbt("w_bf%d" % u, [P, I], BF16)[:] for u in range(HALVES)]
+        val_codes = sbt("val_codes", [P, E], U32)
+        val_scales = sbt("val_scales", [P, E], U8)
 
         def gather_values(j, part, engine):
             n = I // 2
@@ -129,23 +129,25 @@ def tile_attend_beyondgroup_abovepage_blend_pl_kernel(
             else:
                 nc.vector.tensor_copy(val_bf[j][:, part * n : (part + 1) * n], window)
 
-        def turn_pairs(src, turned, grouped):
-            words = src.bitcast(F32)
-            for h in range(2):
-                nc.tensor.transpose(turned[:, h, :], words[:, h : I // 2 : 2], ident[:])
-            nc.scalar.copy(grouped[:].bitcast(F32), turned[:].rearrange("p h c -> p c h"))
-
-        def quantise_values(j):
-            turned = bank("val_turned%d" % j, "vt%d" % (j % 2), [P, 2, P])
-            grouped = sbt("val_grouped%d" % j, [P, P, PACK], BF16)
-            turn_pairs(val_bf[j], turned, grouped)
-            val_codes[j] = sbt("val_codes%d" % j, [P, P], U32)
-            val_scales[j] = sbt("val_scales%d" % j, [P, P], U8)
-            nc.vector.quantize_mx(
-                val_codes[j][:].bitcast(FP8X4), val_scales[j][:], grouped[:].rearrange("p c t -> p (c t)")
+        def turn_pairs(sources, turned, grouped, copy, sorted_pairs=False):
+            for n, src in enumerate(sources):
+                words = src.bitcast(F32)
+                for h in range(2):
+                    picked = words[:, h * P : (h + 1) * P] if sorted_pairs else words[:, h : I // 2 : 2]
+                    nc.tensor.transpose(turned[:, n, h, :], picked, ident[:])
+            copy(
+                grouped.bitcast(F32).rearrange("p (n c h) -> p n c h", n=len(sources), h=2),
+                turned[:].rearrange("p n h c -> p n c h"),
             )
 
-        probs = []
+        def quantise_values(js, tag, grouped, copy):
+            turned = bank("val_turned%d" % js.start, tag, [P, len(js), 2, P])
+            turn_pairs([val_bf[j] for j in js], turned, grouped, copy)
+            for n, j in enumerate(js):
+                es = slice(j * P, (j + 1) * P)
+                nc.vector.quantize_mx(val_codes[:, es].bitcast(FP8X4), val_scales[:, es], grouped[:, n * I : (n + 1) * I])
+
+        scores = []
         for u in range(HALVES):
             neg_sum = neg_sums[u]
             nc.vector.tensor_reduce(
@@ -169,115 +171,116 @@ def tile_attend_beyondgroup_abovepage_blend_pl_kernel(
                 nc.tensor.matmul(
                     score[:, t, :], shift[:, t, :], ident[:], start=False, stop=(t == order[-1]), is_transpose=True
                 )
-            prob = sbt("prob%d" % u, [P, I], F32)
-            nc.scalar.activation(prob[:], score[:].rearrange("p t s -> p (t s)"), ACT.Exp)
-            probs.append(prob)
+            scores.append(score)
 
         for part in range(2):
             gather_values(0, part, "scalar")
+        prob_all = sbt("prob_all", [P, HALVES * I], F32, "val_pool0")
+        probs = [prob_all[:, u * I : (u + 1) * I] for u in range(HALVES)]
+        for u in range(HALVES):
+            nc.scalar.activation(probs[u], scores[u][:].rearrange("p t s -> p (t s)"), ACT.Exp)
         for part in range(2):
             gather_values(1, part, "vector")
 
         cols_ps = bank("cols_ps", "vt1", [P, P])
         nc.tensor.transpose(cols_ps[:], rows[:, 1, :], ident[:])
-        cols = sbt("cols", [P, 10], F32)
-        nc.scalar.copy(cols[:], cols_ps[:, 0:10])
         neg_bar = sbt("neg_bar", [P, HALVES], F32)
         nc.scalar.activation(neg_bar[:], cols_ps[:, 0:2], ACT.Copy, scale=-1.0 / GROUP)
+        cols = share2[:, 2 * P : 2 * P + 10]
+        nc.scalar.copy(cols, cols_ps[:, 0:10])
         os_row = bank("os_row", "os", [P, I])
         for c in range(4):
             nc.tensor.transpose(os_row[:, c * P : (c + 1) * P], cols[:, 4 + c : 5 + c].to_broadcast([P, P]), ident[:])
 
         w_codes = sbt("w_codes", [P, Q], U32)
         w_scales = sbt("w_scales", [P, Q], U8)
+        run_sum = sbt("run_sum", [P, HALVES * runs], F32, "val_pool1")
+        run_sums = [run_sum[:, u * runs : (u + 1) * runs] for u in range(HALVES)]
+        prob_runs = [probs[u].rearrange("p (g c) -> p g c", c=GROUP) for u in range(HALVES)]
         for u in range(HALVES):
-            run_sum = sbt("run_sum%d" % u, [P, I // GROUP], F32)
-            prob_runs = probs[u][:].rearrange("p (g c) -> p g c", c=GROUP)
-            nc.vector.tensor_reduce(run_sum[:], prob_runs, AX.X, ALU.add)
-            above = aboves[u]
+            nc.vector.tensor_reduce(run_sums[u], prob_runs[u], AX.X, ALU.add)
+        for u in range(HALVES):
             nc.vector.scalar_tensor_tensor(
-                above.rearrange("p (g c) -> p g c", c=GROUP),
-                run_sum[:].unsqueeze(2).to_broadcast([P, I // GROUP, GROUP]),
+                aboves[u].rearrange("p (g c) -> p g c", c=GROUP),
+                run_sums[u].unsqueeze(2).to_broadcast([P, runs, GROUP]),
                 neg_bar[:, u : u + 1],
-                prob_runs,
+                prob_runs[u],
                 ALU.mult,
                 ALU.add,
             )
-            part_of = sbt("part_of%d" % u, [P, I], F32)
-            row_sum = sbt("row_sum%d" % u, [P, 1], F32)
-            nc.scalar.activation(part_of[:], above, ACT.Relu, accum_out=row_sum[:])
-            denom = sbt("denom%d" % u, [P, 1], F32)
-            nc.vector.tensor_tensor(denom[:], row_sum[:], cols[:, 2 + u : 3 + u], ALU.add)
-            inverse = sbt("inverse%d" % u, [P, 1], F32)
-            nc.vector.reciprocal(inverse[:], denom[:])
-            w_bf = sbt("w_bf%d" % u, [P, I], BF16)[:]
-            nc.vector.scalar_tensor_tensor(w_bf, part_of[:], inverse[:], os_row[:], ALU.mult, ALU.mult)
-            turned = bank("w_turned%d" % u, "s%d" % u, [P, 2, P])
-            grouped = sbt("w_grouped%d" % u, [P, P, PACK], BF16)
-            turn_pairs(w_bf, turned, grouped)
-            nc.vector.quantize_mx(
-                w_codes[:, u * P : (u + 1) * P].bitcast(FP8X4),
-                w_scales[:, u * P : (u + 1) * P],
-                grouped[:].rearrange("p c t -> p (c t)"),
-            )
-
         for part in range(2):
             gather_values(2, part, "scalar")
-        hold_ps = bank("hold_ps", "vt1", [P, Q])
-        for c in range(HALVES):
-            nc.tensor.transpose(hold_ps[:, c * P : (c + 1) * P], cols[:, 8 + c : 9 + c].to_broadcast([P, P]), ident[:])
-        hold_row = sbt("hold_row", [P, Q], F32)
-        nc.vector.tensor_copy(hold_row[:], hold_ps[:])
-        fresh_row = sbt("fresh_row", [P, Q], F32)
-        nc.gpsimd.tensor_scalar(fresh_row[:], hold_row[:], -1.0, 1.0, ALU.mult, ALU.add)
-        kept = sbt("kept", [P, PACK, Q], F32)
+        part_all = sbt("part_all", [P, (HALVES + 1) * I], F32, "val_pool2")
+        parts = [part_all[:, u * I : (u + 1) * I] for u in range(HALVES)]
+        row_sums = [sbt("row_sum%d" % u, [P, 1], F32) for u in range(HALVES)]
         for u in range(HALVES):
-            qs = slice(u * P, (u + 1) * P)
-            nc.gpsimd.tensor_tensor(
-                kept[:, :, qs], before_sb[:, :, qs], hold_row[:, qs].unsqueeze(1).to_broadcast([P, PACK, P]), ALU.mult
+            nc.scalar.activation(parts[u], aboves[u], ACT.Relu, accum_out=row_sums[u][:])
+        for u in range(HALVES):
+            denom = probs[1][:, 8 * u : 8 * u + 1]
+            nc.vector.tensor_scalar(denom, row_sums[u][:], cols[:, 2 + u : 3 + u], None, ALU.add)
+            inverse = sbt("inverse%d" % u, [P, 1], F32)
+            nc.vector.reciprocal(inverse[:], denom)
+            for h in range(2):
+                nc.vector.scalar_tensor_tensor(
+                    w_bfs[u][:, h * I // 2 : (h + 1) * I // 2].rearrange("p (s e) -> p s e", e=2),
+                    parts[u].rearrange("p (s h e) -> p s h e", h=2, e=2)[:, :, h, :],
+                    inverse[:],
+                    os_row[:].rearrange("p (s h e) -> p s h e", h=2, e=2)[:, :, h, :],
+                    ALU.mult,
+                    ALU.mult,
+                )
+        gather_values(3, 0, "scalar")
+        gather_values(3, 1, "scalar")
+        late = sbt("late", [P, 3 * I], BF16, "val_pool3")
+        w_grouped = [late[:, u * I : (u + 1) * I] for u in range(HALVES)]
+        for u in range(HALVES):
+            turned = bank("w_turned%d" % u, "vt%d" % u, [P, 1, 2, P])
+            grouped = w_grouped[u]
+            turn_pairs([w_bfs[u]], turned, grouped, nc.scalar.copy, True)
+            nc.vector.quantize_mx(
+                w_codes[:, u * P : (u + 1) * P].bitcast(FP8X4), w_scales[:, u * P : (u + 1) * P], grouped
             )
 
-        quantise_values(0)
-        quantise_values(1)
-        quantise_values(2)
-        gather_values(3, 0, "vector")
-        gather_values(3, 1, "scalar")
-        quantise_values(3)
+        hold_ps = bank("hold_ps", "lh", [P, Q])
+        for c in range(HALVES):
+            nc.tensor.transpose(hold_ps[:, c * P : (c + 1) * P], cols[:, 8 + c : 9 + c].to_broadcast([P, P]), ident[:])
+        hold_row = probs[1][:, Q : 2 * Q]
+        nc.vector.tensor_copy(hold_row, hold_ps[:])
+        fresh_row = sbt("fresh_row", [P, Q], F32)
+        nc.gpsimd.tensor_scalar(fresh_row[:], hold_row, -1.0, 1.0, ALU.mult, ALU.add)
+        quantise_values(range(3, 4), "a0", sbt("val_grouped3", [P, I], BF16)[:], nc.scalar.copy)
+        quantise_values(range(0, 2), "s0", part_all[:, 2 * I : 3 * I].bitcast(BF16), nc.scalar.copy)
+        quantise_values(range(2, 3), "s1", parts[1][:, 0 : I // 2].bitcast(BF16), nc.vector.tensor_copy)
+        kept_all = sbt("kept", [P, PACK, Q], F32)
+        for u in range(HALVES):
+            qs = slice(u * P, (u + 1) * P)
+            for j in range(PACK):
+                nc.gpsimd.tensor_tensor(kept_all[:, j, qs], before_sb[:, j, qs], hold_row[:, qs], ALU.mult)
 
         result = sbt("result", [P, PACK, Q], F32)
         out_dealt = out_0.rearrange("(p j) q -> p j q", j=PACK)
-        last = PACK - 1
-        for u in range(HALVES):
-            qs = slice(u * P, (u + 1) * P)
-            read = bank("read%d" % u, "a%d" % u, [P, last, P])
-            for j in range(last):
+
+        def blend(name, tag, js, qs, adder, fresh_tag):
+            shape = [P, js.stop - js.start, qs.stop - qs.start]
+            read = bank("read" + name, tag, shape)
+            for j in range(js.start, js.stop):
                 nc.tensor.matmul_mx(
-                    out=read[:, j, :],
-                    lhsT=val_codes[j][:].bitcast(FP8X4),
-                    lhsT_scale=val_scales[j][:],
+                    out=read[:, j - js.start, :],
+                    lhsT=val_codes[:, j * P : (j + 1) * P].bitcast(FP8X4),
+                    lhsT_scale=val_scales[:, j * P : (j + 1) * P],
                     rhs=w_codes[:, qs].bitcast(FP8X4),
                     rhs_scale=w_scales[:, qs],
                     start=True,
                     stop=True,
                 )
-            fresh = sbt("fresh%d" % u, [P, last, P], F32)
-            nc.vector.tensor_tensor(fresh[:], read[:], fresh_row[:, qs].unsqueeze(1).to_broadcast([P, last, P]), ALU.mult)
-            nc.vector.tensor_tensor(result[:, 0:last, qs], fresh[:], kept[:, 0:last, qs], ALU.add)
-            nc.sync.dma_start(out_dealt[:, 0:last, qs], result[:, 0:last, qs])
-        read = bank("read_last", "lh", [P, Q])
-        nc.tensor.matmul_mx(
-            out=read[:],
-            lhsT=val_codes[last][:].bitcast(FP8X4),
-            lhsT_scale=val_scales[last][:],
-            rhs=w_codes[:].bitcast(FP8X4),
-            rhs_scale=w_scales[:],
-            start=True,
-            stop=True,
-        )
-        fresh = sbt("fresh_last", [P, Q], F32)
-        nc.vector.tensor_tensor(fresh[:], read[:], fresh_row[:], ALU.mult)
-        nc.vector.tensor_tensor(result[:, last, :], fresh[:], kept[:, last, :], ALU.add)
-        nc.sync.dma_start(out_dealt[:, last, :], result[:, last, :])
+            fresh = sbt("fresh" + name, shape, F32, fresh_tag)
+            nc.vector.tensor_tensor(fresh[:], read[:], fresh_row[:, qs].unsqueeze(1).to_broadcast(shape), ALU.mult)
+            adder.tensor_tensor(result[:, js, qs], fresh[:], kept_all[:, js, qs], ALU.add)
+            nc.sync.dma_start(out_dealt[:, js, qs], result[:, js, qs])
+
+        blend("_a", "a1", slice(0, 3), slice(0, P), nc.vector, "fresh0")
+        blend("_b", "lh", slice(3, 4), slice(0, Q), nc.vector, "fresh1")
+        blend("_c", "s0", slice(0, 3), slice(P, Q), nc.vector, "fresh0")
 
         y_codes = sbt("y_codes", [P, Q], U32)
         y_scales = sbt("y_scales", [P, Q], U8)
@@ -286,7 +289,7 @@ def tile_attend_beyondgroup_abovepage_blend_pl_kernel(
             y_bf = sbt("y_bf%d" % u, [P, P, PACK], BF16)
             dst = y_bf[:].rearrange("p (c i) j -> p c j i", i=4)
             src = result[:, :, qs].rearrange("p j (c i) -> p c j i", i=4)
-            if u == 0:
+            if u == 1:
                 nc.vector.tensor_copy(dst, src)
             else:
                 nc.scalar.copy(dst, src)
@@ -295,5 +298,5 @@ def tile_attend_beyondgroup_abovepage_blend_pl_kernel(
         for quad in range(4):
             engine = nc.sync if quad % 2 == 0 else nc.scalar
             engine.dma_start(
-                out_2[0, 4 * quad : 4 * quad + 4, :].bitcast(I32), y_scales[32 * quad : 32 * quad + 4, :].bitcast(I32)
+                out_2[0, quad:16:4, :].bitcast(I32), y_scales[quad:P:32, :].bitcast(I32)
             )

@@ -215,20 +215,29 @@ def tile_attend_beyondgroup_abovepage_blend_pl_kernel(
         row_sums = [sbt("row_sum%d" % u, [P, 1], F32) for u in range(HALVES)]
         for u in range(HALVES):
             nc.scalar.activation(parts[u], aboves[u], ACT.Relu, accum_out=row_sums[u][:])
+        denoms = [probs[1][:, 8 * u : 8 * u + 1] for u in range(HALVES)]
+        inverses = [sbt("inverse%d" % u, [P, 1], F32) for u in range(HALVES)]
+
+        def add_reserve(u):
+            nc.vector.tensor_scalar(denoms[u], row_sums[u][:], cols[:, 2 + u : 3 + u], None, ALU.add)
+
+        def weigh(u, h):
+            nc.vector.scalar_tensor_tensor(
+                w_bfs[u][:, h * I // 2 : (h + 1) * I // 2].rearrange("p (s e) -> p s e", e=2),
+                parts[u].rearrange("p (s h e) -> p s h e", h=2, e=2)[:, :, h, :],
+                inverses[u][:],
+                os_row[:].rearrange("p (s h e) -> p s h e", h=2, e=2)[:, :, h, :],
+                ALU.mult,
+                ALU.mult,
+            )
+
+        add_reserve(0)
+        nc.vector.reciprocal(inverses[0][:], denoms[0])
+        add_reserve(1)
+        nc.vector.reciprocal(inverses[1][:], denoms[1])
         for u in range(HALVES):
-            denom = probs[1][:, 8 * u : 8 * u + 1]
-            nc.vector.tensor_scalar(denom, row_sums[u][:], cols[:, 2 + u : 3 + u], None, ALU.add)
-            inverse = sbt("inverse%d" % u, [P, 1], F32)
-            nc.vector.reciprocal(inverse[:], denom)
             for h in range(2):
-                nc.vector.scalar_tensor_tensor(
-                    w_bfs[u][:, h * I // 2 : (h + 1) * I // 2].rearrange("p (s e) -> p s e", e=2),
-                    parts[u].rearrange("p (s h e) -> p s h e", h=2, e=2)[:, :, h, :],
-                    inverse[:],
-                    os_row[:].rearrange("p (s h e) -> p s h e", h=2, e=2)[:, :, h, :],
-                    ALU.mult,
-                    ALU.mult,
-                )
+                weigh(u, h)
         gather_values(3, 0, "scalar")
         gather_values(3, 1, "scalar")
         late = sbt("late", [P, 3 * I], BF16, "val_pool3")
@@ -278,9 +287,9 @@ def tile_attend_beyondgroup_abovepage_blend_pl_kernel(
             adder.tensor_tensor(result[:, js, qs], fresh[:], kept_all[:, js, qs], ALU.add)
             nc.sync.dma_start(out_dealt[:, js, qs], result[:, js, qs])
 
-        blend("_a", "a1", slice(0, 3), slice(0, P), nc.vector, "fresh0")
+        blend("_a", "a1", slice(0, 3), slice(0, P), nc.gpsimd, "fresh0")
         blend("_b", "lh", slice(3, 4), slice(0, Q), nc.vector, "fresh1")
-        blend("_c", "s0", slice(0, 3), slice(P, Q), nc.vector, "fresh0")
+        blend("_c", "s0", slice(0, 3), slice(P, Q), nc.vector, "fresh2")
 
         y_codes = sbt("y_codes", [P, Q], U32)
         y_scales = sbt("y_scales", [P, Q], U8)

@@ -63,9 +63,10 @@ def tile_attend_beyondgroup_abovepage_blend_pl_kernel(
         nc.sync.dma_start(rows[2:4, 1, :], reserve.rearrange("(u q) o -> u (q o)", u=2))
         nc.sync.dma_start(rows[4:8, 1, :], slot_factor.rearrange("o (u q) -> (o u) q", u=4))
         nc.sync.dma_start(rows[8:10, 1, :], hold.rearrange("o (u q) -> (o u) q", u=2))
-        for j in range(1, PACK):
+        for j in range(1, PACK - 1):
             nc.sync.dma_start(val_pool[j][:], vals_dealt[:, j, :])
         nc.sync.dma_start(before_sb[:], before.rearrange("(p j) q -> p j q", j=PACK))
+        nc.sync.dma_start(val_pool[PACK - 1][:], vals_dealt[:, PACK - 1, :])
 
         keys_g = sbt("keys_g", [P, I], U16)
         key_scale_g = sbt("key_scale_g", [P, I], U8)
@@ -119,7 +120,7 @@ def tile_attend_beyondgroup_abovepage_blend_pl_kernel(
         aboves = [sbt("above0", [P, I], F32)[:], share3[:]]
         w_bfs = [sbt("w_bf%d" % u, [P, I], BF16)[:] for u in range(HALVES)]
         val_codes = sbt("val_codes", [P, E], U32)
-        val_scales = sbt("val_scales", [P, E], U8)
+        val_scales = {}
 
         def gather_values(j, part, engine):
             n = I // 2
@@ -140,12 +141,14 @@ def tile_attend_beyondgroup_abovepage_blend_pl_kernel(
                 turned[:].rearrange("p n h c -> p n c h"),
             )
 
-        def quantise_values(js, tag, grouped, copy):
+        def quantise_values(js, tag, grouped, copy, scale_tag=None):
             turned = bank("val_turned%d" % js.start, tag, [P, len(js), 2, P])
             turn_pairs([val_bf[j] for j in js], turned, grouped, copy)
+            scales = sbt("val_scales%d" % js.start, [P, len(js) * P], U8, scale_tag)
             for n, j in enumerate(js):
                 es = slice(j * P, (j + 1) * P)
-                nc.vector.quantize_mx(val_codes[:, es].bitcast(FP8X4), val_scales[:, es], grouped[:, n * I : (n + 1) * I])
+                val_scales[j] = scales[:, n * P : (n + 1) * P]
+                nc.vector.quantize_mx(val_codes[:, es].bitcast(FP8X4), val_scales[j], grouped[:, n * I : (n + 1) * I])
 
         scores = []
         for u in range(HALVES):
@@ -219,7 +222,7 @@ def tile_attend_beyondgroup_abovepage_blend_pl_kernel(
         inverses = [sbt("inverse%d" % u, [P, 1], F32) for u in range(HALVES)]
 
         def add_reserve(u):
-            nc.vector.tensor_scalar(denoms[u], row_sums[u][:], cols[:, 2 + u : 3 + u], None, ALU.add)
+            nc.vector.tensor_scalar(denoms[u], cols_ps[:, 2 + u : 3 + u], row_sums[u][:], None, ALU.add)
 
         def weigh(u, h):
             nc.vector.scalar_tensor_tensor(
@@ -255,17 +258,14 @@ def tile_attend_beyondgroup_abovepage_blend_pl_kernel(
             nc.tensor.transpose(hold_ps[:, c * P : (c + 1) * P], cols[:, 8 + c : 9 + c].to_broadcast([P, P]), ident[:])
         hold_row = probs[1][:, Q : 2 * Q]
         nc.vector.tensor_copy(hold_row, hold_ps[:])
-        fresh_row = sbt("fresh_row", [P, Q], F32)
-        nc.gpsimd.tensor_scalar(fresh_row[:], hold_row, -1.0, 1.0, ALU.mult, ALU.add)
         quantise_values(range(3, 4), "a0", sbt("val_grouped3", [P, I], BF16)[:], nc.scalar.copy)
-        quantise_values(range(0, 2), "s0", part_all[:, 2 * I : 3 * I].bitcast(BF16), nc.scalar.copy)
         quantise_values(range(2, 3), "s1", parts[1][:, 0 : I // 2].bitcast(BF16), nc.vector.tensor_copy)
+        quantise_values(range(0, 2), "s0", part_all[:, 2 * I : 3 * I].bitcast(BF16), nc.scalar.copy, "inverse1")
         kept_all = sbt("kept", [P, PACK, Q], F32)
-        for u in range(HALVES):
-            qs = slice(u * P, (u + 1) * P)
-            for j in range(PACK):
-                nc.gpsimd.tensor_tensor(kept_all[:, j, qs], before_sb[:, j, qs], hold_row[:, qs], ALU.mult)
+        nc.gpsimd.tensor_tensor(kept_all[:], before_sb[:], hold_row.unsqueeze(1).to_broadcast([P, PACK, Q]), ALU.mult)
 
+        fresh_row = sbt("fresh_row", [P, Q], F32, "before_sb")
+        nc.gpsimd.tensor_scalar(fresh_row[:], hold_row, -1.0, 1.0, ALU.mult, ALU.add)
         result = sbt("result", [P, PACK, Q], F32)
         out_dealt = out_0.rearrange("(p j) q -> p j q", j=PACK)
 
@@ -276,7 +276,7 @@ def tile_attend_beyondgroup_abovepage_blend_pl_kernel(
                 nc.tensor.matmul_mx(
                     out=read[:, j - js.start, :],
                     lhsT=val_codes[:, j * P : (j + 1) * P].bitcast(FP8X4),
-                    lhsT_scale=val_scales[:, j * P : (j + 1) * P],
+                    lhsT_scale=val_scales[j],
                     rhs=w_codes[:, qs].bitcast(FP8X4),
                     rhs_scale=w_scales[:, qs],
                     start=True,

from contextlib import ExitStack

import concourse.mybir as mybir
from concourse.masks import make_identity

D, T, I, Q, E = 512, 2048, 512, 256, 512
FLOPS = 2 * D * I * Q + 2 * I * E * Q

F32 = mybir.dt.float32
BF16 = mybir.dt.bfloat16
I32 = mybir.dt.int32
U32 = mybir.dt.uint32
U16 = mybir.dt.uint16
U8 = mybir.dt.uint8
FP8X4 = mybir.dt.float8_e4m3fn_x4
FP4X4 = mybir.dt.float4_e2m1fn_x4
ALU = mybir.AluOpType
ACT = mybir.ActivationFunctionType
AX = mybir.AxisListType

P = 128
PACK = 4
GROUP = 8
HALVES = Q // P


def tile_attend_beyondgroup_abovepage_blend_pl_kernel(
    tc, query, keys_words, keys_scales, lam, bar, reserve, slot_factor, vals, before, hold, offs, out_0, out_1, out_2
):
    nc = tc.nc
    with ExitStack() as ctx:
        sb = ctx.enter_context(tc.tile_pool(name="sb", bufs=1))
        ps = ctx.enter_context(tc.psum_pool(name="ps", bufs=1))

        def sbt(name, shape, dtype, tag=None):
            return sb.tile(shape, dtype, name=name, tag=tag or name, align_bytes=64)

        def bank(name, tag, shape):
            return ps.tile(shape, F32, name=name, tag=tag)

        offsets = sb.tile([P, I // 16], U16, name="offsets")
        key_words = sbt("key_words", [P, T], U16)
        key_bytes = sbt("key_bytes", [P, T], U8)
        rows = sbt("rows", [P, 2, P], F32)
        q_raw = sbt("q_raw", [P, PACK, Q], F32)
        before_sb = sbt("before_sb", [P, PACK, Q], F32)
        val_pool = [sbt("val_pool%d" % j, [P, T], F32) for j in range(PACK)]
        ident = sbt("ident", [P, P], F32)

        nc.gpsimd.memset(key_bytes[:].bitcast(I32), 0)
        nc.gpsimd.memset(rows[:], 0.0)
        make_identity(nc, ident[:])

        nc.sync.dma_start(offsets[:], offs)
        nc.sync.dma_start(key_words[:].bitcast(I32), keys_words[0].bitcast(I32))
        for r in range(4):
            nc.sync.dma_start(key_bytes[r:P:32, :].bitcast(I32), keys_scales[0, r:16:4, :].bitcast(I32))
        nc.sync.dma_start(q_raw[:], query.rearrange("(p j) q -> p j q", j=PACK))
        vals_dealt = vals.rearrange("(p j) t -> p j t", j=PACK)
        nc.sync.dma_start(rows[0:2, 0, :], lam.rearrange("o (u q) -> (o u) q", u=2))
        nc.sync.dma_start(val_pool[0][:], vals_dealt[:, 0, :])
        nc.sync.dma_start(rows[0:2, 1, :], bar.rearrange("(u q) o -> u (q o)", u=2))
        nc.sync.dma_start(rows[2:4, 1, :], reserve.rearrange("(u q) o -> u (q o)", u=2))
        nc.sync.dma_start(rows[4:8, 1, :], slot_factor.rearrange("o (u q) -> (o u) q", u=4))
        nc.sync.dma_start(rows[8:10, 1, :], hold.rearrange("o (u q) -> (o u) q", u=2))
        for j in range(1, PACK - 1):
            nc.sync.dma_start(val_pool[j][:], vals_dealt[:, j, :])
        nc.sync.dma_start(before_sb[:], before.rearrange("(p j) q -> p j q", j=PACK))
        nc.sync.dma_start(val_pool[PACK - 1][:], vals_dealt[:, PACK - 1, :])

        keys_g = sbt("keys_g", [P, I], U16)
        key_scale_g = sbt("key_scale_g", [P, I], U8)
        nc.vector.tensor_copy(keys_g[:], key_words[:].indirect(offsets[:]))
        nc.vector.tensor_copy(key_scale_g[:], key_bytes[:].indirect(offsets[:]))

        lam_ps = bank("lam_ps", "vt0", [P, P])
        nc.tensor.transpose(lam_ps[:], rows[:, 0, :], ident[:])
        lam_cols = sbt("lam_cols", [P, HALVES], F32)
        nc.scalar.copy(lam_cols[:], lam_ps[:, 0:HALVES])
        lam_row = bank("lam_row", "lh", [P, Q])
        for c in range(HALVES):
            nc.tensor.transpose(lam_row[:, c * P : (c + 1) * P], lam_cols[:, c : c + 1].to_broadcast([P, P]), ident[:])

        q_codes, q_scales = [], []
        for u in range(HALVES):
            q_bf = sbt("q_bf%d" % u, [P, P, PACK], BF16)
            nc.scalar.copy(
                q_bf[:].rearrange("p (c i) j -> p c j i", i=4),
                q_raw[:, :, u * P : (u + 1) * P].rearrange("p j (c i) -> p c j i", i=4),
            )
            codes = sbt("q_codes%d" % u, [P, P], U32)
            scales = sbt("q_scales%d" % u, [P, P], U8)
            nc.vector.quantize_mx(codes[:].bitcast(FP8X4), scales[:], q_bf[:].rearrange("p q j -> p (q j)"))
            q_codes.append(codes)
            q_scales.append(scales)

        raw_ps = []
        for u in range(HALVES):
            raw = bank("raw%d" % u, "a%d" % u, [P, PACK, P])
            for t in range(PACK):
                nc.tensor.matmul_mx(
                    out=raw[:, t, :],
                    lhsT=keys_g[:, t * P : (t + 1) * P].bitcast(FP4X4),
                    lhsT_scale=key_scale_g[:, t * P : (t + 1) * P],
                    rhs=q_codes[u][:].bitcast(FP8X4),
                    rhs_scale=q_scales[u][:],
                    start=True,
                    stop=True,
                )
            raw_ps.append(raw)

        runs = I // GROUP
        share0 = sbt("share0", [P, I // 2], F32)
        share2 = sbt("share2", [P, I + P // 2], F32)
        share3 = sbt("share3", [P, I], F32)
        val_bf = [share0[:].bitcast(BF16), sbt("val_bf1", [P, I], BF16)[:]]
        val_bf += [share2[:, I + P // 2 - I // 2 : I + P // 2].bitcast(BF16), share3[:, 0 : I // 2].bitcast(BF16)]
        neg_sums = [share0[:, P : P + runs], sbt("neg_sum1", [P, runs], F32)[:]]
        shifts = [sbt("shift0", [P, I], F32)[:], share2[:, 0:I]]
        aboves = [sbt("above0", [P, I], F32)[:], share3[:]]
        w_bfs = [sbt("w_bf%d" % u, [P, I], BF16)[:] for u in range(HALVES)]
        val_codes = sbt("val_codes", [P, E], U32)
        val_scales = {}

        def gather_values(j, part, engine):
            n = I // 2
            window = val_pool[j][:].indirect(offsets[:, part * n // 16 : (part + 1) * n // 16])
            if engine == "scalar":
                nc.scalar.activation(val_bf[j][:, part * n : (part + 1) * n], window, ACT.Copy)
            else:
                nc.vector.tensor_copy(val_bf[j][:, part * n : (part + 1) * n], window)

        def turn_pairs(sources, turned, grouped, copy, sorted_pairs=False):
            for n, src in enumerate(sources):
                words = src.bitcast(F32)
                for h in range(2):
                    picked = words[:, h * P : (h + 1) * P] if sorted_pairs else words[:, h : I // 2 : 2]
                    nc.tensor.transpose(turned[:, n, h, :], picked, ident[:])
            copy(
                grouped.bitcast(F32).rearrange("p (n c h) -> p n c h", n=len(sources), h=2),
                turned[:].rearrange("p n h c -> p n c h"),
            )

        def quantise_values(js, tag, grouped, copy, scale_tag=None):
            turned = bank("val_turned%d" % js.start, tag, [P, len(js), 2, P])
            turn_pairs([val_bf[j] for j in js], turned, grouped, copy)
            scales = sbt("val_scales%d" % js.start, [P, len(js) * P], U8, scale_tag)
            for n, j in enumerate(js):
                es = slice(j * P, (j + 1) * P)
                val_scales[j] = scales[:, n * P : (n + 1) * P]
                nc.vector.quantize_mx(val_codes[:, es].bitcast(FP8X4), val_scales[j], grouped[:, n * I : (n + 1) * I])

        scores = []
        for u in range(HALVES):
            neg_sum = neg_sums[u]
            nc.vector.tensor_reduce(
                neg_sum, raw_ps[u][:].rearrange("p t (v c) -> p (t v) c", c=GROUP), AX.X, ALU.add, negate=True
            )
            raw_sb = sbt("raw_sb%d" % u, [P, PACK, P], F32)
            nc.scalar.copy(raw_sb[:], raw_ps[u][:])
            shift = shifts[u].rearrange("p (t q) -> p t q", t=PACK)
            four_d = [P, PACK, P // GROUP, GROUP]
            nc.vector.tensor_tensor(
                shift.rearrange("p t (v c) -> p t v c", c=GROUP),
                neg_sum.rearrange("p (t v) -> p t v", t=PACK).unsqueeze(3).to_broadcast(four_d),
                lam_row[:, u * P : (u + 1) * P].rearrange("p (v c) -> p v c", c=GROUP).unsqueeze(1).to_broadcast(four_d),
                ALU.mult,
            )
            score = bank("score%d" % u, "s%d" % u, [P, PACK, P])
            for t in range(PACK):
                nc.tensor.matmul(score[:, t, :], raw_sb[:, t, :], ident[:], start=(t == 0), stop=False, is_transpose=True)
            order = list(range(PACK))
            for t in order:
                nc.tensor.matmul(
                    score[:, t, :], shift[:, t, :], ident[:], start=False, stop=(t == order[-1]), is_transpose=True
                )
            scores.append(score)

        for part in range(2):
            gather_values(0, part, "scalar")
        prob_all = sbt("prob_all", [P, HALVES * I], F32, "val_pool0")
        probs = [prob_all[:, u * I : (u + 1) * I] for u in range(HALVES)]
        for u in range(HALVES):
            nc.scalar.activation(probs[u], scores[u][:].rearrange("p t s -> p (t s)"), ACT.Exp)
        for part in range(2):
            gather_values(1, part, "vector")

        cols_ps = bank("cols_ps", "vt1", [P, P])
        nc.tensor.transpose(cols_ps[:], rows[:, 1, :], ident[:])
        neg_bar = sbt("neg_bar", [P, HALVES], F32)
        nc.scalar.activation(neg_bar[:], cols_ps[:, 0:2], ACT.Copy, scale=-1.0 / GROUP)
        cols = share2[:, 2 * P : 2 * P + 10]
        nc.scalar.copy(cols, cols_ps[:, 0:10])
        os_row = bank("os_row", "os", [P, I])
        for c in range(4):
            nc.tensor.transpose(os_row[:, c * P : (c + 1) * P], cols[:, 4 + c : 5 + c].to_broadcast([P, P]), ident[:])

        w_codes = sbt("w_codes", [P, Q], U32)
        w_scales = sbt("w_scales", [P, Q], U8)
        run_sum = sbt("run_sum", [P, HALVES * runs], F32, "val_pool1")
        run_sums = [run_sum[:, u * runs : (u + 1) * runs] for u in range(HALVES)]
        prob_runs = [probs[u].rearrange("p (g c) -> p g c", c=GROUP) for u in range(HALVES)]
        for u in range(HALVES):
            nc.vector.tensor_reduce(run_sums[u], prob_runs[u], AX.X, ALU.add)
        for u in range(HALVES):
            nc.vector.scalar_tensor_tensor(
                aboves[u].rearrange("p (g c) -> p g c", c=GROUP),
                run_sums[u].unsqueeze(2).to_broadcast([P, runs, GROUP]),
                neg_bar[:, u : u + 1],
                prob_runs[u],
                ALU.mult,
                ALU.add,
            )
        for part in range(2):
            gather_values(2, part, "scalar")
        part_all = sbt("part_all", [P, (HALVES + 1) * I], F32, "val_pool2")
        parts = [part_all[:, u * I : (u + 1) * I] for u in range(HALVES)]
        row_sums = [sbt("row_sum%d" % u, [P, 1], F32) for u in range(HALVES)]
        for u in range(HALVES):
            nc.scalar.activation(parts[u], aboves[u], ACT.Relu, accum_out=row_sums[u][:])
        denoms = [probs[1][:, 8 * u : 8 * u + 1] for u in range(HALVES)]
        inverses = [sbt("inverse%d" % u, [P, 1], F32) for u in range(HALVES)]

        def add_reserve(u):
            nc.vector.tensor_scalar(denoms[u], cols_ps[:, 2 + u : 3 + u], row_sums[u][:], None, ALU.add)

        def weigh(u, h):
            nc.vector.scalar_tensor_tensor(
                w_bfs[u][:, h * I // 2 : (h + 1) * I // 2].rearrange("p (s e) -> p s e", e=2),
                parts[u].rearrange("p (s h e) -> p s h e", h=2, e=2)[:, :, h, :],
                inverses[u][:],
                os_row[:].rearrange("p (s h e) -> p s h e", h=2, e=2)[:, :, h, :],
                ALU.mult,
                ALU.mult,
            )

        add_reserve(0)
        nc.vector.reciprocal(inverses[0][:], denoms[0])
        add_reserve(1)
        nc.vector.reciprocal(inverses[1][:], denoms[1])
        for u in range(HALVES):
            for h in range(2):
                weigh(u, h)
        gather_values(3, 0, "scalar")
        gather_values(3, 1, "scalar")
        late = sbt("late", [P, 3 * I], BF16, "val_pool3")
        w_grouped = [late[:, u * I : (u + 1) * I] for u in range(HALVES)]
        for u in range(HALVES):
            turned = bank("w_turned%d" % u, "vt%d" % u, [P, 1, 2, P])
            grouped = w_grouped[u]
            turn_pairs([w_bfs[u]], turned, grouped, nc.scalar.copy, True)
            nc.vector.quantize_mx(
                w_codes[:, u * P : (u + 1) * P].bitcast(FP8X4), w_scales[:, u * P : (u + 1) * P], grouped
            )

        hold_ps = bank("hold_ps", "lh", [P, Q])
        for c in range(HALVES):
            nc.tensor.transpose(hold_ps[:, c * P : (c + 1) * P], cols[:, 8 + c : 9 + c].to_broadcast([P, P]), ident[:])
        hold_row = probs[1][:, Q : 2 * Q]
        nc.vector.tensor_copy(hold_row, hold_ps[:])
        quantise_values(range(3, 4), "a0", sbt("val_grouped3", [P, I], BF16)[:], nc.scalar.copy)
        quantise_values(range(2, 3), "s1", parts[1][:, 0 : I // 2].bitcast(BF16), nc.vector.tensor_copy)
        quantise_values(range(0, 2), "s0", part_all[:, 2 * I : 3 * I].bitcast(BF16), nc.scalar.copy, "inverse1")
        kept_all = sbt("kept", [P, PACK, Q], F32)
        nc.gpsimd.tensor_tensor(kept_all[:], before_sb[:], hold_row.unsqueeze(1).to_broadcast([P, PACK, Q]), ALU.mult)

        fresh_row = sbt("fresh_row", [P, Q], F32, "before_sb")
        nc.gpsimd.tensor_scalar(fresh_row[:], hold_row, -1.0, 1.0, ALU.mult, ALU.add)
        result = sbt("result", [P, PACK, Q], F32)
        out_dealt = out_0.rearrange("(p j) q -> p j q", j=PACK)

        def blend(name, tag, js, qs, adder, fresh_tag):
            shape = [P, js.stop - js.start, qs.stop - qs.start]
            read = bank("read" + name, tag, shape)
            for j in range(js.start, js.stop):
                nc.tensor.matmul_mx(
                    out=read[:, j - js.start, :],
                    lhsT=val_codes[:, j * P : (j + 1) * P].bitcast(FP8X4),
                    lhsT_scale=val_scales[j],
                    rhs=w_codes[:, qs].bitcast(FP8X4),
                    rhs_scale=w_scales[:, qs],
                    start=True,
                    stop=True,
                )
            fresh = sbt("fresh" + name, shape, F32, fresh_tag)
            nc.vector.tensor_tensor(fresh[:], read[:], fresh_row[:, qs].unsqueeze(1).to_broadcast(shape), ALU.mult)
            adder.tensor_tensor(result[:, js, qs], fresh[:], kept_all[:, js, qs], ALU.add)
            nc.sync.dma_start(out_dealt[:, js, qs], result[:, js, qs])

        blend("_a", "a1", slice(0, 3), slice(0, P), nc.gpsimd, "fresh0")
        blend("_b", "lh", slice(3, 4), slice(0, Q), nc.vector, "fresh1")
        blend("_c", "s0", slice(0, 3), slice(P, Q), nc.vector, "fresh2")

        y_codes = sbt("y_codes", [P, Q], U32)
        y_scales = sbt("y_scales", [P, Q], U8)
        for u in range(HALVES):
            qs = slice(u * P, (u + 1) * P)
            y_bf = sbt("y_bf%d" % u, [P, P, PACK], BF16)
            dst = y_bf[:].rearrange("p (c i) j -> p c j i", i=4)
            src = result[:, :, qs].rearrange("p j (c i) -> p c j i", i=4)
            if u == 1:
                nc.vector.tensor_copy(dst, src)
            else:
                nc.scalar.copy(dst, src)
            nc.vector.quantize_mx(y_codes[:, qs].bitcast(FP8X4), y_scales[:, qs], y_bf[:].rearrange("p q j -> p (q j)"))
        nc.sync.dma_start(out_1[0].rearrange("p c r -> p (c r)").bitcast(I32), y_codes[:].bitcast(I32))
        for quad in range(4):
            engine = nc.sync if quad % 2 == 0 else nc.scalar
            engine.dma_start(
                out_2[0, quad:16:4, :].bitcast(I32), y_scales[quad:P:32, :].bitcast(I32)
            )
